import numpy as np
import ml_dtypes


def mxq(x, axis, fmt="e4m3"):
    dtype, down = {"e4m3": (ml_dtypes.float8_e4m3fn, 7), "e5m2": (ml_dtypes.float8_e5m2, 14)}[fmt]
    v = np.moveaxis(np.asarray(x, np.float32).astype(ml_dtypes.bfloat16).astype(np.float64), axis, -1)
    blocks = v.reshape(v.shape[:-1] + (-1, 32))
    amax = np.abs(blocks).max(-1, keepdims=True)
    byte = np.maximum(np.where(amax > 0, np.frexp(amax)[1] - 1 + 127, 0) - down, 1)
    scale = np.exp2(byte - 127.0)
    codes = (blocks / scale).astype(np.float32).astype(dtype).astype(np.float64)
    return np.moveaxis((codes * scale).reshape(v.shape), -1, axis)


WIDE = False


def mx_kscale(k):
    if not WIDE:
        return np.ones(k)
    levels = np.array([10, -10, 5, -5, 0])
    if k % 512:
        return np.exp2(np.random.permutation(np.resize(levels, k // 32))).repeat(32)
    a = np.empty((k // 512, 16))
    for p in range(k // 512):
        a[p, :8] = np.random.permutation(np.resize(levels, 8))
        for g in range(8):
            far = levels[np.abs(levels - a[p, g]) >= 10]
            a[p, g + 8] = far[np.random.randint(len(far))]
    return np.exp2(a.ravel()).repeat(32)


def f64(x):
    return np.asarray(x).astype(np.float64)


def striped(idx):
    return np.tile(np.asarray(idx).reshape(-1, 16).T, (8, 1)).astype(np.uint16)


def unstriped(offs):
    return offs[:16].T.reshape(-1).astype(np.int64)


E2M1 = np.array([0.0, 0.5, 1.0, 1.5, 2.0, 3.0, 4.0, 6.0, -0.0, -0.5, -1.0, -1.5, -2.0, -3.0, -4.0, -6.0])


def pack_weight(w, fmt):
    k, n = w.shape
    w = f64(np.asarray(w, np.float32).astype(ml_dtypes.bfloat16)).reshape(k // 32, 32, n)
    amax = np.abs(w).max(1)
    if fmt == "e4m3":
        byte = np.frexp(amax)[1] - 1 + 127 - 7
    else:
        mant, ex = np.frexp(amax / 6.0)
        byte = np.where(mant > 0.5, ex, ex - 1) + 127
    byte = np.clip(np.where(amax > 0, byte, 1), 1, 254)
    scaled = (w * np.exp2(127.0 - byte)[:, None, :]).reshape(k, n).astype(np.float32)
    by_word = np.ascontiguousarray(scaled.reshape(k // 512, 128, 4, n).transpose(0, 1, 3, 2))
    if fmt == "e4m3":
        words = by_word.astype(ml_dtypes.float8_e4m3fn).view(np.uint8)
    else:
        c = by_word.astype(ml_dtypes.float4_e2m1fn).view(np.uint8) & 0xF
        words = (c[..., 0::2] | (c[..., 1::2] << 4)).reshape(k // 512, 128, 2 * n)
    return np.ascontiguousarray(words), np.ascontiguousarray(byte.astype(np.uint8).reshape(k // 512, 16, n))


def unpack_weight(words, scales, fmt):
    g, _, n = scales.shape
    words = np.ascontiguousarray(words).reshape(g, 128, n, -1)
    if fmt == "e4m3":
        vals = words.view(ml_dtypes.float8_e4m3fn).astype(np.float64)
    else:
        nib = np.empty((g, 128, n, 4), np.uint8)
        nib[..., 0::2] = words & 0xF
        nib[..., 1::2] = words >> 4
        vals = E2M1[nib]
    vals = vals * np.repeat(np.exp2(scales.astype(np.float64) - 127.0), 8, axis=1)[..., None]
    return vals.transpose(0, 1, 3, 2).reshape(g * 512, n)


def sigmoid(v):
    return 1.0 / (1.0 + np.exp(-v))


D, E, T, I, Q, G = 512, 512, 2048, 512, 128, 64


def setup_inputs():
    n = np.random.standard_normal
    idx = np.random.permutation(T)[:I]
    fd = mx_kscale(D)
    fe = mx_kscale(E)
    keysp = pack_weight(n((D, T)) / fd[:, None], "e4m3")
    valsp = pack_weight(n((E, T)) / fe[:, None], "e4m3")
    return {
        "query": (n((D, Q)) * 0.6 / np.sqrt(D) * fd[:, None]).astype(np.float32),
        "keys_words": keysp[0],
        "keys_scales": keysp[1],
        "gout": (n((E, Q)) * 1 / np.sqrt(E) * fe[:, None]).astype(np.float32),
        "vals_words": valsp[0],
        "vals_scales": valsp[1],
        "size": (np.random.uniform(0.5, 2.0, (1, I))).astype(np.float32),
        "dquery": (n((D, Q)) * 1.0 / np.sqrt(D) * fd[:, None]).astype(np.float32),
        "base": (0.5 * n((Q, T))).astype(np.float32),
        "offs": striped(idx),
    }


def reference(query, keys_words, keys_scales, gout, vals_words, vals_scales, size, dquery, base, offs):
    idx = unstriped(offs)
    keysu = unpack_weight(keys_words, keys_scales, "e4m3")
    valsu = unpack_weight(vals_words, vals_scales, "e4m3")
    queryq = mxq(f64(query), 0, "e4m3")
    keysidxg = keysu[:, idx]
    a = queryq.T @ keysidxg
    dqueryq = mxq(f64(dquery), 0, "e4m3")
    ta = dqueryq.T @ keysidxg
    s = a.reshape(Q, G, I // G).mean(axis=2)
    p = np.exp(s - np.max(s, axis=1, keepdims=True))
    z = np.sum(p, axis=1, keepdims=True)
    r = p / z
    rr = np.repeat(r, I // G, axis=1)
    goutq = mxq(f64(gout), 0, "e4m3")
    valsidxg = valsu[:, idx]
    c0 = goutq.T @ valsidxg
    drr = c0 * f64(size) * sigmoid(a)
    dr = drr.reshape(Q, G, I // G).sum(axis=2)
    dz = np.sum(dr * p / np.square(z) * (-1.0), axis=1, keepdims=True)
    dp = dr / z + dz
    ts = ta.reshape(Q, G, I // G).mean(axis=2)
    tp = ts * p
    tz = np.sum(tp, axis=1, keepdims=True)
    tr = (tp - tz * p / z) / z
    trr = np.repeat(tr, I // G, axis=1)
    tdrr = ta * sigmoid(a) * (1.0 - sigmoid(a)) * c0 * f64(size)
    tdr = tdrr.reshape(Q, G, I // G).sum(axis=2)
    tdz = np.sum((tdr * p + tp * dr - tz * z * 2.0 * dr * p / np.square(z)) / np.square(z) * (-1.0), axis=1, keepdims=True)
    tdp = (tdr - tz * dr / z) / z + tdz
    tds = tdp * p + tp * dp
    te1 = tds / 8.0
    tr1 = np.repeat(te1, I // G, axis=1)
    tda = (trr * c0 * f64(size) * sigmoid(a) + ta * sigmoid(a) * (1.0 - sigmoid(a)) * c0 * f64(size) * rr) * (1.0 - sigmoid(a)) + ta * sigmoid(a) * (1.0 - sigmoid(a)) * (-1.0) * c0 * f64(size) * rr * sigmoid(a) + tr1
    gs = tda * 512.0
    gf = np.zeros((Q, T))
    gf[:, idx] = gs
    y = f64(base) + gf
    return y

@@ -1,0 +1,223 @@
+from contextlib import ExitStack
+
+import concourse.mybir as mybir
+from concourse.masks import make_identity
+
+D, E, T, I, Q, G = 512, 512, 2048, 512, 128, 64
+SPAN = I // G
+FLOPS = 3 * 2 * 512 * Q * I
+
+F32 = mybir.dt.float32
+BF16 = mybir.dt.bfloat16
+I32 = mybir.dt.int32
+U32 = mybir.dt.uint32
+U16 = mybir.dt.uint16
+U8 = mybir.dt.uint8
+FP8X4 = mybir.dt.float8_e4m3fn_x4
+ALU = mybir.AluOpType
+ACT = mybir.ActivationFunctionType
+AX = mybir.AxisListType
+
+P = 128
+PACK = 4
+OUT_CHUNK = 512
+KIB = 1024
+AT_BASE = 0
+AT_VAL_POOL = 4 * KIB
+AT_TA_T = 8 * KIB
+AT_KEY_SCALES = 11 * KIB
+AT_KEY_CODES = 12 * KIB
+AT_QUERY = 14 * KIB
+AT_VAL_SCALES = 14 * KIB
+AT_SIZE = 16 * KIB
+AT_DQUERY = 16 * KIB
+AT_GOUT = 17 * KIB
+AT_KEY_POOL = 19 * KIB
+
+
+def tile_attend_hvspanread_s_kernel(
+    tc, query, keys_words, keys_scales, gout, vals_words, vals_scales, size, dquery, base, offs, out
+):
+    nc = tc.nc
+    with ExitStack() as ctx:
+        keep = ctx.enter_context(tc.tile_pool(name="keep", bufs=1))
+        shared = ctx.enter_context(tc.tile_pool(name="shared", bufs=1))
+        psum = ctx.enter_context(tc.psum_pool(name="psum", bufs=1))
+
+        def by_span(ap):
+            return ap.rearrange("p (g j) -> p g j", j=SPAN)
+
+        def over_span(ap):
+            return ap.unsqueeze(2).to_broadcast([P, G, SPAN])
+
+        def load_words(words, name, offset):
+            pool_words = shared.tile([P, T], U32, name=name, offset=offset, align_bytes=64)
+            nc.sync.dma_start(
+                out=pool_words[:].bitcast(I32), in_=words[0].rearrange("p n t -> p (n t)").bitcast(I32)
+            )
+            return pool_words
+
+        def load_scales(scales, name, offset):
+            pool_scales = shared.tile([P, T], U8, name=name, offset=offset, align_bytes=64)
+            nc.vector.memset(pool_scales[:].bitcast(I32), 0)
+            for quad in range(4):
+                nc.scalar.dma_start(
+                    out=pool_scales[32 * quad : 32 * quad + 4, :].bitcast(I32),
+                    in_=scales[0, 4 * quad : 4 * quad + 4, :].bitcast(I32),
+                )
+            return pool_scales
+
+        def load_rows(rows, name, offset):
+            raw = shared.tile([P, PACK, Q], F32, name=name, offset=offset, align_bytes=64)
+            nc.sync.dma_start(out=raw[:], in_=rows.rearrange("(p j) w -> p j w", j=PACK))
+            return raw
+
+        def interleave(raw, name):
+            grouped = keep.tile([P, Q, PACK], BF16, name=name, align_bytes=64)
+            nc.scalar.activation(grouped[:], raw[:].rearrange("p j w -> p w j"), ACT.Copy)
+            return grouped
+
+        def quantise(grouped, name):
+            codes = keep.tile([P, Q], U32, name=name + "_codes", align_bytes=64)
+            scales = keep.tile([P, Q], U8, name=name + "_scales", align_bytes=64)
+            nc.vector.quantize_mx(
+                out=codes[:].bitcast(FP8X4), scales=scales[:], in_=grouped[:].rearrange("p w j -> p (w j)")
+            )
+            return codes, scales
+
+        def gather(window, picked):
+            nc.vector.tensor_copy(picked[:], window[:].indirect(offsets[:]))
+            return picked
+
+        offsets = keep.tile([P, I // 16], U16, name="offsets")
+        nc.sync.dma_start(offsets[:], offs)
+        query_raw = load_rows(query, "query_raw", AT_QUERY)
+        key_pool = load_words(keys_words, "key_pool", AT_KEY_POOL)
+        dquery_raw = load_rows(dquery, "dquery_raw", AT_DQUERY)
+        key_pool_scales = load_scales(keys_scales, "key_pool_scales", AT_KEY_SCALES)
+
+        window = keep.tile([P, T], F32, name="window")
+        nc.vector.memset(window[:], 0.0)
+        ident = keep.tile([P, P], F32, name="ident")
+        make_identity(nc, ident[:])
+
+        query_grouped = interleave(query_raw, "query_grouped")
+        key_scales = gather(key_pool_scales, keep.tile([P, I], U8, name="key_scales", align_bytes=64))
+        val_pool = load_words(vals_words, "val_pool", AT_VAL_POOL)
+        val_pool_scales = load_scales(vals_scales, "val_pool_scales", AT_VAL_SCALES)
+        key_codes = gather(
+            key_pool, shared.tile([P, I], U32, name="key_codes", offset=AT_KEY_CODES, align_bytes=64)
+        )
+
+        dquery_grouped = interleave(dquery_raw, "dquery_grouped")
+        gout_raw = load_rows(gout, "gout_raw", AT_GOUT)
+        size_rows = shared.tile([P, P], F32, name="size_rows", offset=AT_SIZE, align_bytes=64)
+        nc.gpsimd.memset(size_rows[:], 0.0)
+        nc.sync.dma_start(out=size_rows[0:4, :], in_=size.rearrange("o (k p) -> (o k) p", p=P))
+
+        query_codes, query_scales = quantise(query_grouped, "query")
+        a_ps = psum.tile([P, I], F32, name="a_ps")
+        nc.tensor.matmul_mx(
+            out=a_ps[:], lhsT=query_codes[:].bitcast(FP8X4), lhsT_scale=query_scales[:],
+            rhs=key_codes[:].bitcast(FP8X4), rhs_scale=key_scales[:], start=True, stop=True,
+        )
+        dquery_codes, dquery_scales = quantise(dquery_grouped, "dquery")
+        ta_ps = psum.tile([P, I], F32, name="ta_ps")
+        nc.tensor.matmul_mx(
+            out=ta_ps[:], lhsT=dquery_codes[:].bitcast(FP8X4), lhsT_scale=dquery_scales[:],
+            rhs=key_codes[:].bitcast(FP8X4), rhs_scale=key_scales[:], start=True, stop=True,
+        )
+
+        a_sum = keep.tile([P, G], F32, name="a_sum")
+        nc.vector.tensor_reduce(a_sum[:], by_span(a_ps[:]), AX.X, ALU.add)
+        neg_s = keep.tile([P, G], F32, name="neg_s")
+        neg_max = keep.tile([P, 1], F32, name="neg_max")
+        nc.vector.tensor_scalar(neg_s[:], a_sum[:], -1.0 / SPAN, None, ALU.mult, ALU.min, accum_out=neg_max[:])
+        ta_sum = keep.tile([P, G], F32, name="ta_sum")
+        nc.vector.tensor_reduce(ta_sum[:], by_span(ta_ps[:]), AX.X, ALU.add)
+
+        t = keep.tile([P, I], F32, name="t")
+        nc.scalar.activation(t[:], a_ps[:], ACT.Tanh, scale=0.5)
+        p = keep.tile([P, G], F32, name="p")
+        z = keep.tile([P, 1], F32, name="z")
+        nc.scalar.activation(p[:], neg_s[:], ACT.Exp, bias=neg_max[:], scale=-1.0, accum_out=z[:])
+        gout_grouped = interleave(gout_raw, "gout_grouped")
+        tsq4 = keep.tile([P, I], F32, name="tsq4")
+        nc.scalar.activation(tsq4[:], t[:], ACT.Square, scale=2.0)
+
+        size_ps = psum.tile([P, P], F32, name="size_ps")
+        nc.tensor.transpose(size_ps[:], size_rows[:], ident[:])
+        size_cols = keep.tile([P, 4], F32, name="size_cols")
+        nc.scalar.activation(size_cols[:], size_ps[:, 0:4], ACT.Copy, scale=32.0)
+
+        val_scales = gather(val_pool_scales, keep.tile([P, I], U8, name="val_scales", align_bytes=64))
+        val_codes = gather(val_pool, keep.tile([P, I], U32, name="val_codes", align_bytes=64))
+        base_sb = shared.tile([P, T], F32, name="base_sb", offset=AT_BASE, align_bytes=64)
+        nc.sync.dma_start(out=base_sb[:], in_=base)
+        gout_codes, gout_scales = quantise(gout_grouped, "gout")
+        cs_ps = psum.tile([P, I], F32, name="cs_ps")
+        cs_turned = keep.tile([P, 4, Q], F32, name="cs_turned")
+        for k in range(4):
+            cols = slice(P * k, P * (k + 1))
+            c0_ps = psum.tile([P, Q], F32, name="c0_ps%d" % k)
+            nc.tensor.matmul_mx(
+                out=c0_ps[:], lhsT=val_codes[:, cols].bitcast(FP8X4), lhsT_scale=val_scales[:, cols],
+                rhs=gout_codes[:].bitcast(FP8X4), rhs_scale=gout_scales[:], start=True, stop=True,
+            )
+            nc.scalar.activation(cs_turned[:, k, :], c0_ps[:], ACT.Copy, scale=size_cols[:, k : k + 1])
+        for k in range(4):
+            nc.tensor.transpose(cs_ps[:, P * k : P * (k + 1)], cs_turned[:, k, :], ident[:])
+
+        inv_z = keep.tile([P, 1], F32, name="inv_z")
+        nc.vector.reciprocal(inv_z[:], z[:])
+        ta_t = shared.tile([P, I], F32, name="ta_t", offset=AT_TA_T, align_bytes=64)
+        nc.vector.tensor_tensor(ta_t[:], ta_ps[:], t[:], ALU.mult)
+        r_ta = keep.tile([P, G], F32, name="r_ta")
+        mean_sum = keep.tile([P, 1], F32, name="mean_sum")
+        nc.vector.scalar_tensor_tensor(
+            r_ta[:], ta_sum[:], inv_z[:], p[:], ALU.mult, ALU.mult, accum_out=mean_sum[:]
+        )
+        centred = keep.tile([P, G], F32, name="centred")
+        nc.vector.tensor_scalar(centred[:], ta_sum[:], mean_sum[:], 1.0 / SPAN, ALU.subtract, ALU.mult)
+        share = keep.tile([P, I], F32, name="share")
+        nc.scalar.activation(by_span(share[:]), over_span(p[:]), ACT.Copy, scale=inv_z[:])
+        bend = keep.tile([P, I], F32, name="bend")
+        nc.vector.tensor_tensor(by_span(bend[:]), by_span(ta_t[:]), over_span(centred[:]), ALU.subtract)
+
+        drr2 = keep.tile([P, I], F32, name="drr2")
+        nc.vector.scalar_tensor_tensor(drr2[:], t[:], 1.0, cs_ps[:], ALU.add, ALU.mult)
+        slope = keep.tile([P, I], F32, name="slope")
+        nc.vector.scalar_tensor_tensor(slope[:], tsq4[:], 4.0, cs_ps[:], ALU.subtract, ALU.mult)
+        dr2 = keep.tile([P, G], F32, name="dr2")
+        nc.vector.tensor_reduce(dr2[:], by_span(drr2[:]), AX.X, ALU.add)
+        tdrr = keep.tile([P, I], F32, name="tdrr")
+        nc.vector.tensor_tensor(tdrr[:], ta_ps[:], slope[:], ALU.mult)
+        r_dr = keep.tile([P, G], F32, name="r_dr")
+        mean_dr = keep.tile([P, 1], F32, name="mean_dr")
+        nc.vector.scalar_tensor_tensor(
+            r_dr[:], dr2[:], inv_z[:], p[:], ALU.mult, ALU.mult, accum_out=mean_dr[:]
+        )
+        tdr = keep.tile([P, G], F32, name="tdr")
+        nc.vector.tensor_reduce(tdr[:], by_span(tdrr[:]), AX.X, ALU.add)
+        cross = keep.tile([P, G], F32, name="cross")
+        nc.vector.scalar_tensor_tensor(cross[:], dr2[:], mean_dr[:], centred[:], ALU.subtract, ALU.mult)
+        w = keep.tile([P, G], F32, name="w")
+        nc.vector.scalar_tensor_tensor(w[:], tdr[:], -0.125, cross[:], ALU.mult, ALU.add)
+        local = keep.tile([P, I], F32, name="local")
+        nc.vector.tensor_tensor(local[:], slope[:], bend[:], ALU.mult)
+        r_w = keep.tile([P, G], F32, name="r_w")
+        mean_w = keep.tile([P, 1], F32, name="mean_w")
+        nc.vector.scalar_tensor_tensor(
+            r_w[:], w[:], inv_z[:], p[:], ALU.mult, ALU.mult, accum_out=mean_w[:]
+        )
+        total = keep.tile([P, I], F32, name="total")
+        nc.vector.scalar_tensor_tensor(
+            by_span(total[:]), over_span(w[:]), mean_w[:], by_span(local[:]), ALU.subtract, ALU.add
+        )
+        nc.vector.tensor_tensor(window[:].indirect(offsets[:]), total[:], share[:], ALU.mult)
+
+        for c in range(T // OUT_CHUNK):
+            cols = slice(OUT_CHUNK * c, OUT_CHUNK * (c + 1))
+            result = keep.tile([P, OUT_CHUNK], F32, name="result%d" % c)
+            nc.vector.tensor_tensor(result[:], window[:, cols], base_sb[:, cols], ALU.add)
+            nc.sync.dma_start(out=out[:, cols], in_=result[:])

@@ -22,17 +22,21 @@ P = 128
 PACK = 4
 OUT_CHUNK = 512
 KIB = 1024
-AT_BASE = 0
-AT_VAL_POOL = 4 * KIB
-AT_TA_T = 8 * KIB
-AT_KEY_SCALES = 11 * KIB
-AT_KEY_CODES = 12 * KIB
-AT_QUERY = 14 * KIB
-AT_VAL_SCALES = 14 * KIB
-AT_SIZE = 16 * KIB
-AT_DQUERY = 16 * KIB
-AT_GOUT = 17 * KIB
-AT_KEY_POOL = 19 * KIB
+AT_VAL_POOL = 0
+AT_TA_T = 0
+AT_QUERY = 7 * KIB
+AT_GOUT = 8 * KIB
+AT_DQUERY = 10 * KIB
+AT_SIZE = 10 * KIB
+AT_KEY_SCALES = 12 * KIB
+AT_VAL_SCALES = 29 * KIB
+AT_BASE = 16 * KIB
+AT_KEY_POOL = 20 * KIB
+AT_A_SUM = 30 * KIB
+AT_VAL_CODES = AT_A_SUM + 128 - 2 * KIB
+AT_GOUT_CODES = AT_A_SUM + 128
+AT_VAL_PICKED = 24 * KIB
+OUT_CHUNKS = (512, 512, 512, 256, 256)
 
 
 def tile_attend_hvspanread_s_kernel(
@@ -57,11 +61,11 @@ def tile_attend_hvspanread_s_kernel(
             )
             return pool_words
 
-        def load_scales(scales, name, offset):
+        def load_scales(scales, name, offset, queue):
             pool_scales = shared.tile([P, T], U8, name=name, offset=offset, align_bytes=64)
             nc.vector.memset(pool_scales[:].bitcast(I32), 0)
             for quad in range(4):
-                nc.scalar.dma_start(
+                queue.dma_start(
                     out=pool_scales[32 * quad : 32 * quad + 4, :].bitcast(I32),
                     in_=scales[0, 4 * quad : 4 * quad + 4, :].bitcast(I32),
                 )
@@ -77,8 +81,8 @@ def tile_attend_hvspanread_s_kernel(
             nc.scalar.activation(grouped[:], raw[:].rearrange("p j w -> p w j"), ACT.Copy)
             return grouped
 
-        def quantise(grouped, name):
-            codes = keep.tile([P, Q], U32, name=name + "_codes", align_bytes=64)
+        def quantise(grouped, name, offset):
+            codes = shared.tile([P, Q], U32, name=name + "_codes", offset=offset, align_bytes=64)
             scales = keep.tile([P, Q], U8, name=name + "_scales", align_bytes=64)
             nc.vector.quantize_mx(
                 out=codes[:].bitcast(FP8X4), scales=scales[:], in_=grouped[:].rearrange("p w j -> p (w j)")
@@ -92,43 +96,43 @@ def tile_attend_hvspanread_s_kernel(
         offsets = keep.tile([P, I // 16], U16, name="offsets")
         nc.sync.dma_start(offsets[:], offs)
         query_raw = load_rows(query, "query_raw", AT_QUERY)
-        key_pool = load_words(keys_words, "key_pool", AT_KEY_POOL)
         dquery_raw = load_rows(dquery, "dquery_raw", AT_DQUERY)
-        key_pool_scales = load_scales(keys_scales, "key_pool_scales", AT_KEY_SCALES)
-
-        window = keep.tile([P, T], F32, name="window")
-        nc.vector.memset(window[:], 0.0)
+        key_pool = load_words(keys_words, "key_pool", AT_KEY_POOL)
+        key_pool_scales = load_scales(keys_scales, "key_pool_scales", AT_KEY_SCALES, nc.scalar)
+        val_pool_scales = load_scales(vals_scales, "val_pool_scales", AT_VAL_SCALES, nc.gpsimd)
         ident = keep.tile([P, P], F32, name="ident")
         make_identity(nc, ident[:])
+        window = keep.tile([P, T], F32, name="window")
+        nc.vector.memset(window[:], 0.0)
 
         query_grouped = interleave(query_raw, "query_grouped")
-        key_scales = gather(key_pool_scales, keep.tile([P, I], U8, name="key_scales", align_bytes=64))
-        val_pool = load_words(vals_words, "val_pool", AT_VAL_POOL)
-        val_pool_scales = load_scales(vals_scales, "val_pool_scales", AT_VAL_SCALES)
-        key_codes = gather(
-            key_pool, shared.tile([P, I], U32, name="key_codes", offset=AT_KEY_CODES, align_bytes=64)
-        )
-
-        dquery_grouped = interleave(dquery_raw, "dquery_grouped")
         gout_raw = load_rows(gout, "gout_raw", AT_GOUT)
+        val_pool = load_words(vals_words, "val_pool", AT_VAL_POOL)
+        dquery_grouped = interleave(dquery_raw, "dquery_grouped")
         size_rows = shared.tile([P, P], F32, name="size_rows", offset=AT_SIZE, align_bytes=64)
-        nc.gpsimd.memset(size_rows[:], 0.0)
+        nc.vector.memset(size_rows[:], 0.0)
         nc.sync.dma_start(out=size_rows[0:4, :], in_=size.rearrange("o (k p) -> (o k) p", p=P))
 
-        query_codes, query_scales = quantise(query_grouped, "query")
+        key_scales = gather(key_pool_scales, keep.tile([P, I], U8, name="key_scales", align_bytes=64))
+        query_codes, query_scales = quantise(query_grouped, "query", 12 * KIB + 2 * KIB)
+        dquery_codes, dquery_scales = quantise(dquery_grouped, "dquery", 15 * KIB)
+        key_codes = gather(key_pool, shared.tile([P, I], U32, name="key_codes", offset=AT_KEY_SCALES, align_bytes=64))
+        base_sb = shared.tile([P, T], F32, name="base_sb", offset=AT_BASE, align_bytes=64)
+        nc.sync.dma_start(out=base_sb[:], in_=base)
+
         a_ps = psum.tile([P, I], F32, name="a_ps")
         nc.tensor.matmul_mx(
             out=a_ps[:], lhsT=query_codes[:].bitcast(FP8X4), lhsT_scale=query_scales[:],
             rhs=key_codes[:].bitcast(FP8X4), rhs_scale=key_scales[:], start=True, stop=True,
         )
-        dquery_codes, dquery_scales = quantise(dquery_grouped, "dquery")
         ta_ps = psum.tile([P, I], F32, name="ta_ps")
         nc.tensor.matmul_mx(
             out=ta_ps[:], lhsT=dquery_codes[:].bitcast(FP8X4), lhsT_scale=dquery_scales[:],
             rhs=key_codes[:].bitcast(FP8X4), rhs_scale=key_scales[:], start=True, stop=True,
         )
 
-        a_sum = keep.tile([P, G], F32, name="a_sum")
+        val_scales = gather(val_pool_scales, shared.tile([P, I], U8, name="val_scales", offset=AT_VAL_PICKED, align_bytes=64))
+        a_sum = shared.tile([P, G], F32, name="a_sum", offset=AT_A_SUM, align_bytes=64)
         nc.vector.tensor_reduce(a_sum[:], by_span(a_ps[:]), AX.X, ALU.add)
         neg_s = keep.tile([P, G], F32, name="neg_s")
         neg_max = keep.tile([P, 1], F32, name="neg_max")
@@ -150,11 +154,8 @@ def tile_attend_hvspanread_s_kernel(
         size_cols = keep.tile([P, 4], F32, name="size_cols")
         nc.scalar.activation(size_cols[:], size_ps[:, 0:4], ACT.Copy, scale=32.0)
 
-        val_scales = gather(val_pool_scales, keep.tile([P, I], U8, name="val_scales", align_bytes=64))
-        val_codes = gather(val_pool, keep.tile([P, I], U32, name="val_codes", align_bytes=64))
-        base_sb = shared.tile([P, T], F32, name="base_sb", offset=AT_BASE, align_bytes=64)
-        nc.sync.dma_start(out=base_sb[:], in_=base)
-        gout_codes, gout_scales = quantise(gout_grouped, "gout")
+        val_codes = gather(val_pool, shared.tile([P, I], U32, name="val_codes", offset=AT_VAL_CODES, align_bytes=64))
+        gout_codes, gout_scales = quantise(gout_grouped, "gout", AT_GOUT_CODES)
         cs_ps = psum.tile([P, I], F32, name="cs_ps")
         cs_turned = keep.tile([P, 4, Q], F32, name="cs_turned")
         for k in range(4):
@@ -216,8 +217,10 @@ def tile_attend_hvspanread_s_kernel(
         )
         nc.vector.tensor_tensor(window[:].indirect(offsets[:]), total[:], share[:], ALU.mult)
 
-        for c in range(T // OUT_CHUNK):
-            cols = slice(OUT_CHUNK * c, OUT_CHUNK * (c + 1))
-            result = keep.tile([P, OUT_CHUNK], F32, name="result%d" % c)
+        start = 0
+        for width in OUT_CHUNKS:
+            cols = slice(start, start + width)
+            result = keep.tile([P, width], F32, name="result%d" % start)
             nc.vector.tensor_tensor(result[:], window[:, cols], base_sb[:, cols], ALU.add)
             nc.sync.dma_start(out=out[:, cols], in_=result[:])
+            start = start + width

@@ -23,19 +23,18 @@ PACK = 4
 OUT_CHUNK = 512
 KIB = 1024
 AT_VAL_POOL = 0
-AT_TA_T = 0
-AT_QUERY = 7 * KIB
+AT_STAGED = (7 * KIB, 32 * KIB, 34 * KIB, 36 * KIB)
 AT_GOUT = 8 * KIB
+AT_SIZE = 36 * KIB
 AT_DQUERY = 10 * KIB
-AT_SIZE = 10 * KIB
 AT_KEY_SCALES = 12 * KIB
-AT_VAL_SCALES = 29 * KIB
+AT_QUERY = 14 * KIB
 AT_BASE = 16 * KIB
 AT_KEY_POOL = 20 * KIB
-AT_A_SUM = 30 * KIB
-AT_VAL_CODES = AT_A_SUM + 128 - 2 * KIB
-AT_GOUT_CODES = AT_A_SUM + 128
-AT_VAL_PICKED = 24 * KIB
+AT_VAL_SCALES = 29 * KIB
+AT_QUERY_GROUPED = 38 * KIB
+AT_DQUERY_GROUPED = 39 * KIB
+AT_GOUT_GROUPED = 40 * KIB
 OUT_CHUNKS = (512, 512, 512, 256, 256)
 
 
@@ -76,13 +75,13 @@ def tile_attend_hvspanread_s_kernel(
             nc.sync.dma_start(out=raw[:], in_=rows.rearrange("(p j) w -> p j w", j=PACK))
             return raw
 
-        def interleave(raw, name):
-            grouped = keep.tile([P, Q, PACK], BF16, name=name, align_bytes=64)
+        def interleave(raw, name, offset):
+            grouped = shared.tile([P, Q, PACK], BF16, name=name, offset=offset, align_bytes=64)
             nc.scalar.activation(grouped[:], raw[:].rearrange("p j w -> p w j"), ACT.Copy)
             return grouped
 
-        def quantise(grouped, name, offset):
-            codes = shared.tile([P, Q], U32, name=name + "_codes", offset=offset, align_bytes=64)
+        def quantise(grouped, name):
+            codes = keep.tile([P, Q], U32, name=name + "_codes", align_bytes=64)
             scales = keep.tile([P, Q], U8, name=name + "_scales", align_bytes=64)
             nc.vector.quantize_mx(
                 out=codes[:].bitcast(FP8X4), scales=scales[:], in_=grouped[:].rearrange("p w j -> p (w j)")
@@ -95,67 +94,77 @@ def tile_attend_hvspanread_s_kernel(
 
         offsets = keep.tile([P, I // 16], U16, name="offsets")
         nc.sync.dma_start(offsets[:], offs)
+        staged = []
+        for quad in range(4):
+            rows = shared.tile([P, T // 4], I32, name="staged%d" % quad, offset=AT_STAGED[quad], align_bytes=64)
+            nc.sync.dma_start(
+                out=rows[32 * quad : 32 * quad + 4, :], in_=keys_scales[0, 4 * quad : 4 * quad + 4, :].bitcast(I32)
+            )
+            staged.append(rows)
+        key_pool = load_words(keys_words, "key_pool", AT_KEY_POOL)
         query_raw = load_rows(query, "query_raw", AT_QUERY)
         dquery_raw = load_rows(dquery, "dquery_raw", AT_DQUERY)
-        key_pool = load_words(keys_words, "key_pool", AT_KEY_POOL)
-        key_pool_scales = load_scales(keys_scales, "key_pool_scales", AT_KEY_SCALES, nc.scalar)
-        val_pool_scales = load_scales(vals_scales, "val_pool_scales", AT_VAL_SCALES, nc.gpsimd)
+        val_pool_scales = load_scales(vals_scales, "val_pool_scales", AT_VAL_SCALES, nc.sync)
+        key_pool_scales = shared.tile([P, T], U8, name="key_pool_scales", offset=AT_KEY_SCALES, align_bytes=64)
+        nc.vector.memset(key_pool_scales[:].bitcast(I32), 0)
         ident = keep.tile([P, P], F32, name="ident")
         make_identity(nc, ident[:])
         window = keep.tile([P, T], F32, name="window")
         nc.vector.memset(window[:], 0.0)
-
-        query_grouped = interleave(query_raw, "query_grouped")
-        gout_raw = load_rows(gout, "gout_raw", AT_GOUT)
+        for quad in range(4):
+            part = slice(32 * quad, 32 * quad + 4)
+            nc.vector.tensor_copy(key_pool_scales[part, :].bitcast(I32), staged[quad][part, :])
         val_pool = load_words(vals_words, "val_pool", AT_VAL_POOL)
-        dquery_grouped = interleave(dquery_raw, "dquery_grouped")
+        gout_raw = load_rows(gout, "gout_raw", AT_GOUT)
         size_rows = shared.tile([P, P], F32, name="size_rows", offset=AT_SIZE, align_bytes=64)
-        nc.vector.memset(size_rows[:], 0.0)
+        nc.gpsimd.memset(size_rows[:], 0.0)
         nc.sync.dma_start(out=size_rows[0:4, :], in_=size.rearrange("o (k p) -> (o k) p", p=P))
 
         key_scales = gather(key_pool_scales, keep.tile([P, I], U8, name="key_scales", align_bytes=64))
-        query_codes, query_scales = quantise(query_grouped, "query", 12 * KIB + 2 * KIB)
-        dquery_codes, dquery_scales = quantise(dquery_grouped, "dquery", 15 * KIB)
-        key_codes = gather(key_pool, shared.tile([P, I], U32, name="key_codes", offset=AT_KEY_SCALES, align_bytes=64))
+        key_codes = gather(key_pool, keep.tile([P, I], U32, name="key_codes", align_bytes=64))
         base_sb = shared.tile([P, T], F32, name="base_sb", offset=AT_BASE, align_bytes=64)
         nc.sync.dma_start(out=base_sb[:], in_=base)
+        query_grouped = interleave(query_raw, "query_grouped", AT_QUERY_GROUPED)
+        dquery_grouped = interleave(dquery_raw, "dquery_grouped", AT_DQUERY_GROUPED)
+        query_codes, query_scales = quantise(query_grouped, "query")
 
         a_ps = psum.tile([P, I], F32, name="a_ps")
         nc.tensor.matmul_mx(
             out=a_ps[:], lhsT=query_codes[:].bitcast(FP8X4), lhsT_scale=query_scales[:],
             rhs=key_codes[:].bitcast(FP8X4), rhs_scale=key_scales[:], start=True, stop=True,
         )
+        val_scales = gather(val_pool_scales, keep.tile([P, I], U8, name="val_scales", align_bytes=64))
+        dquery_codes, dquery_scales = quantise(dquery_grouped, "dquery")
         ta_ps = psum.tile([P, I], F32, name="ta_ps")
         nc.tensor.matmul_mx(
             out=ta_ps[:], lhsT=dquery_codes[:].bitcast(FP8X4), lhsT_scale=dquery_scales[:],
             rhs=key_codes[:].bitcast(FP8X4), rhs_scale=key_scales[:], start=True, stop=True,
         )
 
-        val_scales = gather(val_pool_scales, shared.tile([P, I], U8, name="val_scales", offset=AT_VAL_PICKED, align_bytes=64))
-        a_sum = shared.tile([P, G], F32, name="a_sum", offset=AT_A_SUM, align_bytes=64)
-        nc.vector.tensor_reduce(a_sum[:], by_span(a_ps[:]), AX.X, ALU.add)
-        neg_s = keep.tile([P, G], F32, name="neg_s")
-        neg_max = keep.tile([P, 1], F32, name="neg_max")
-        nc.vector.tensor_scalar(neg_s[:], a_sum[:], -1.0 / SPAN, None, ALU.mult, ALU.min, accum_out=neg_max[:])
-        ta_sum = keep.tile([P, G], F32, name="ta_sum")
-        nc.vector.tensor_reduce(ta_sum[:], by_span(ta_ps[:]), AX.X, ALU.add)
-
         t = keep.tile([P, I], F32, name="t")
         nc.scalar.activation(t[:], a_ps[:], ACT.Tanh, scale=0.5)
-        p = keep.tile([P, G], F32, name="p")
-        z = keep.tile([P, 1], F32, name="z")
-        nc.scalar.activation(p[:], neg_s[:], ACT.Exp, bias=neg_max[:], scale=-1.0, accum_out=z[:])
-        gout_grouped = interleave(gout_raw, "gout_grouped")
+        gout_grouped = interleave(gout_raw, "gout_grouped", AT_GOUT_GROUPED)
+        ta_sb = keep.tile([P, I], F32, name="ta_sb")
+        nc.scalar.copy(ta_sb[:], ta_ps[:])
         tsq4 = keep.tile([P, I], F32, name="tsq4")
         nc.scalar.activation(tsq4[:], t[:], ACT.Square, scale=2.0)
-
         size_ps = psum.tile([P, P], F32, name="size_ps")
         nc.tensor.transpose(size_ps[:], size_rows[:], ident[:])
         size_cols = keep.tile([P, 4], F32, name="size_cols")
         nc.scalar.activation(size_cols[:], size_ps[:, 0:4], ACT.Copy, scale=32.0)
 
-        val_codes = gather(val_pool, shared.tile([P, I], U32, name="val_codes", offset=AT_VAL_CODES, align_bytes=64))
-        gout_codes, gout_scales = quantise(gout_grouped, "gout", AT_GOUT_CODES)
+        val_codes = gather(val_pool, keep.tile([P, I], U32, name="val_codes", align_bytes=64))
+        gout_codes, gout_scales = quantise(gout_grouped, "gout")
+        a_sum = shared.tile([P, G], F32, name="a_sum", offset=AT_VAL_POOL + KIB, align_bytes=64)
+        nc.vector.tensor_reduce(a_sum[:], by_span(a_ps[:]), AX.X, ALU.add)
+        neg_s = keep.tile([P, G], F32, name="neg_s")
+        neg_max = keep.tile([P, 1], F32, name="neg_max")
+        nc.vector.tensor_scalar(neg_s[:], a_sum[:], -1.0 / SPAN, None, ALU.mult, ALU.min, accum_out=neg_max[:])
+
+        p = keep.tile([P, G], F32, name="p")
+        z = keep.tile([P, 1], F32, name="z")
+        nc.scalar.activation(p[:], neg_s[:], ACT.Exp, bias=neg_max[:], scale=-1.0, accum_out=z[:])
+
         cs_ps = psum.tile([P, I], F32, name="cs_ps")
         cs_turned = keep.tile([P, 4, Q], F32, name="cs_turned")
         for k in range(4):
@@ -169,10 +178,12 @@ def tile_attend_hvspanread_s_kernel(
         for k in range(4):
             nc.tensor.transpose(cs_ps[:, P * k : P * (k + 1)], cs_turned[:, k, :], ident[:])
 
+        ta_sum = shared.tile([P, G], F32, name="ta_sum", offset=AT_VAL_POOL, align_bytes=64)
+        nc.vector.tensor_reduce(ta_sum[:], by_span(ta_ps[:]), AX.X, ALU.add)
         inv_z = keep.tile([P, 1], F32, name="inv_z")
         nc.vector.reciprocal(inv_z[:], z[:])
-        ta_t = shared.tile([P, I], F32, name="ta_t", offset=AT_TA_T, align_bytes=64)
-        nc.vector.tensor_tensor(ta_t[:], ta_ps[:], t[:], ALU.mult)
+        ta_t = shared.tile([P, I], F32, name="ta_t", offset=AT_GOUT_GROUPED, align_bytes=64)
+        nc.gpsimd.tensor_tensor(ta_t[:], ta_sb[:], t[:], ALU.mult)
         r_ta = keep.tile([P, G], F32, name="r_ta")
         mean_sum = keep.tile([P, 1], F32, name="mean_sum")
         nc.vector.scalar_tensor_tensor(
@@ -183,7 +194,7 @@ def tile_attend_hvspanread_s_kernel(
         share = keep.tile([P, I], F32, name="share")
         nc.scalar.activation(by_span(share[:]), over_span(p[:]), ACT.Copy, scale=inv_z[:])
         bend = keep.tile([P, I], F32, name="bend")
-        nc.vector.tensor_tensor(by_span(bend[:]), by_span(ta_t[:]), over_span(centred[:]), ALU.subtract)
+        nc.gpsimd.tensor_tensor(by_span(bend[:]), by_span(ta_t[:]), over_span(centred[:]), ALU.subtract)
 
         drr2 = keep.tile([P, I], F32, name="drr2")
         nc.vector.scalar_tensor_tensor(drr2[:], t[:], 1.0, cs_ps[:], ALU.add, ALU.mult)
@@ -205,7 +216,7 @@ def tile_attend_hvspanread_s_kernel(
         w = keep.tile([P, G], F32, name="w")
         nc.vector.scalar_tensor_tensor(w[:], tdr[:], -0.125, cross[:], ALU.mult, ALU.add)
         local = keep.tile([P, I], F32, name="local")
-        nc.vector.tensor_tensor(local[:], slope[:], bend[:], ALU.mult)
+        nc.gpsimd.tensor_tensor(local[:], slope[:], bend[:], ALU.mult)
         r_w = keep.tile([P, G], F32, name="r_w")
         mean_w = keep.tile([P, 1], F32, name="mean_w")
         nc.vector.scalar_tensor_tensor(

from contextlib import ExitStack

import concourse.mybir as mybir
from concourse.masks import make_identity

D, E, T, I, Q, G = 512, 512, 2048, 512, 128, 64
SPAN = I // G
FLOPS = 3 * 2 * 512 * Q * I

F32 = mybir.dt.float32
BF16 = mybir.dt.bfloat16
I32 = mybir.dt.int32
U32 = mybir.dt.uint32
U16 = mybir.dt.uint16
U8 = mybir.dt.uint8
FP8X4 = mybir.dt.float8_e4m3fn_x4
ALU = mybir.AluOpType
ACT = mybir.ActivationFunctionType
AX = mybir.AxisListType

P = 128
PACK = 4
OUT_CHUNK = 512
KIB = 1024
AT_VAL_POOL = 0
AT_STAGED = (7 * KIB, 32 * KIB, 34 * KIB, 36 * KIB)
AT_GOUT = 8 * KIB
AT_SIZE = 36 * KIB
AT_DQUERY = 10 * KIB
AT_KEY_SCALES = 12 * KIB
AT_QUERY = 14 * KIB
AT_BASE = 16 * KIB
AT_KEY_POOL = 20 * KIB
AT_VAL_SCALES = 29 * KIB
AT_QUERY_GROUPED = 38 * KIB
AT_DQUERY_GROUPED = 39 * KIB
AT_GOUT_GROUPED = 40 * KIB
OUT_CHUNKS = (512, 512, 512, 256, 256)


def tile_attend_hvspanread_s_kernel(
    tc, query, keys_words, keys_scales, gout, vals_words, vals_scales, size, dquery, base, offs, out
):
    nc = tc.nc
    with ExitStack() as ctx:
        keep = ctx.enter_context(tc.tile_pool(name="keep", bufs=1))
        shared = ctx.enter_context(tc.tile_pool(name="shared", bufs=1))
        psum = ctx.enter_context(tc.psum_pool(name="psum", bufs=1))

        def by_span(ap):
            return ap.rearrange("p (g j) -> p g j", j=SPAN)

        def over_span(ap):
            return ap.unsqueeze(2).to_broadcast([P, G, SPAN])

        def load_words(words, name, offset):
            pool_words = shared.tile([P, T], U32, name=name, offset=offset, align_bytes=64)
            nc.sync.dma_start(
                out=pool_words[:].bitcast(I32), in_=words[0].rearrange("p n t -> p (n t)").bitcast(I32)
            )
            return pool_words

        def load_scales(scales, name, offset, queue):
            pool_scales = shared.tile([P, T], U8, name=name, offset=offset, align_bytes=64)
            nc.vector.memset(pool_scales[:].bitcast(I32), 0)
            for quad in range(4):
                queue.dma_start(
                    out=pool_scales[32 * quad : 32 * quad + 4, :].bitcast(I32),
                    in_=scales[0, 4 * quad : 4 * quad + 4, :].bitcast(I32),
                )
            return pool_scales

        def load_rows(rows, name, offset):
            raw = shared.tile([P, PACK, Q], F32, name=name, offset=offset, align_bytes=64)
            nc.sync.dma_start(out=raw[:], in_=rows.rearrange("(p j) w -> p j w", j=PACK))
            return raw

        def interleave(raw, name, offset):
            grouped = shared.tile([P, Q, PACK], BF16, name=name, offset=offset, align_bytes=64)
            nc.scalar.activation(grouped[:], raw[:].rearrange("p j w -> p w j"), ACT.Copy)
            return grouped

        def quantise(grouped, name):
            codes = keep.tile([P, Q], U32, name=name + "_codes", align_bytes=64)
            scales = keep.tile([P, Q], U8, name=name + "_scales", align_bytes=64)
            nc.vector.quantize_mx(
                out=codes[:].bitcast(FP8X4), scales=scales[:], in_=grouped[:].rearrange("p w j -> p (w j)")
            )
            return codes, scales

        def gather(window, picked):
            nc.vector.tensor_copy(picked[:], window[:].indirect(offsets[:]))
            return picked

        offsets = keep.tile([P, I // 16], U16, name="offsets")
        nc.sync.dma_start(offsets[:], offs)
        staged = []
        for quad in range(4):
            rows = shared.tile([P, T // 4], I32, name="staged%d" % quad, offset=AT_STAGED[quad], align_bytes=64)
            nc.sync.dma_start(
                out=rows[32 * quad : 32 * quad + 4, :], in_=keys_scales[0, 4 * quad : 4 * quad + 4, :].bitcast(I32)
            )
            staged.append(rows)
        key_pool = load_words(keys_words, "key_pool", AT_KEY_POOL)
        query_raw = load_rows(query, "query_raw", AT_QUERY)
        dquery_raw = load_rows(dquery, "dquery_raw", AT_DQUERY)
        val_pool_scales = load_scales(vals_scales, "val_pool_scales", AT_VAL_SCALES, nc.sync)
        key_pool_scales = shared.tile([P, T], U8, name="key_pool_scales", offset=AT_KEY_SCALES, align_bytes=64)
        nc.vector.memset(key_pool_scales[:].bitcast(I32), 0)
        ident = keep.tile([P, P], F32, name="ident")
        make_identity(nc, ident[:])
        window = keep.tile([P, T], F32, name="window")
        nc.vector.memset(window[:], 0.0)
        for quad in range(4):
            part = slice(32 * quad, 32 * quad + 4)
            nc.vector.tensor_copy(key_pool_scales[part, :].bitcast(I32), staged[quad][part, :])
        val_pool = load_words(vals_words, "val_pool", AT_VAL_POOL)
        gout_raw = load_rows(gout, "gout_raw", AT_GOUT)
        size_rows = shared.tile([P, P], F32, name="size_rows", offset=AT_SIZE, align_bytes=64)
        nc.gpsimd.memset(size_rows[:], 0.0)
        nc.sync.dma_start(out=size_rows[0:4, :], in_=size.rearrange("o (k p) -> (o k) p", p=P))

        key_scales = gather(key_pool_scales, keep.tile([P, I], U8, name="key_scales", align_bytes=64))
        key_codes = gather(key_pool, keep.tile([P, I], U32, name="key_codes", align_bytes=64))
        base_sb = shared.tile([P, T], F32, name="base_sb", offset=AT_BASE, align_bytes=64)
        nc.sync.dma_start(out=base_sb[:], in_=base)
        query_grouped = interleave(query_raw, "query_grouped", AT_QUERY_GROUPED)
        dquery_grouped = interleave(dquery_raw, "dquery_grouped", AT_DQUERY_GROUPED)
        query_codes, query_scales = quantise(query_grouped, "query")

        a_ps = psum.tile([P, I], F32, name="a_ps")
        nc.tensor.matmul_mx(
            out=a_ps[:], lhsT=query_codes[:].bitcast(FP8X4), lhsT_scale=query_scales[:],
            rhs=key_codes[:].bitcast(FP8X4), rhs_scale=key_scales[:], start=True, stop=True,
        )
        val_scales = gather(val_pool_scales, keep.tile([P, I], U8, name="val_scales", align_bytes=64))
        dquery_codes, dquery_scales = quantise(dquery_grouped, "dquery")
        ta_ps = psum.tile([P, I], F32, name="ta_ps")
        nc.tensor.matmul_mx(
            out=ta_ps[:], lhsT=dquery_codes[:].bitcast(FP8X4), lhsT_scale=dquery_scales[:],
            rhs=key_codes[:].bitcast(FP8X4), rhs_scale=key_scales[:], start=True, stop=True,
        )

        t = keep.tile([P, I], F32, name="t")
        nc.scalar.activation(t[:], a_ps[:], ACT.Tanh, scale=0.5)
        gout_grouped = interleave(gout_raw, "gout_grouped", AT_GOUT_GROUPED)
        ta_sb = keep.tile([P, I], F32, name="ta_sb")
        nc.scalar.copy(ta_sb[:], ta_ps[:])
        tsq4 = keep.tile([P, I], F32, name="tsq4")
        nc.scalar.activation(tsq4[:], t[:], ACT.Square, scale=2.0)
        size_ps = psum.tile([P, P], F32, name="size_ps")
        nc.tensor.transpose(size_ps[:], size_rows[:], ident[:])
        size_cols = keep.tile([P, 4], F32, name="size_cols")
        nc.scalar.activation(size_cols[:], size_ps[:, 0:4], ACT.Copy, scale=32.0)

        val_codes = gather(val_pool, keep.tile([P, I], U32, name="val_codes", align_bytes=64))
        gout_codes, gout_scales = quantise(gout_grouped, "gout")
        a_sum = shared.tile([P, G], F32, name="a_sum", offset=AT_VAL_POOL + KIB, align_bytes=64)
        nc.vector.tensor_reduce(a_sum[:], by_span(a_ps[:]), AX.X, ALU.add)
        neg_s = keep.tile([P, G], F32, name="neg_s")
        neg_max = keep.tile([P, 1], F32, name="neg_max")
        nc.vector.tensor_scalar(neg_s[:], a_sum[:], -1.0 / SPAN, None, ALU.mult, ALU.min, accum_out=neg_max[:])

        p = keep.tile([P, G], F32, name="p")
        z = keep.tile([P, 1], F32, name="z")
        nc.scalar.activation(p[:], neg_s[:], ACT.Exp, bias=neg_max[:], scale=-1.0, accum_out=z[:])

        cs_ps = psum.tile([P, I], F32, name="cs_ps")
        cs_turned = keep.tile([P, 4, Q], F32, name="cs_turned")
        for k in range(4):
            cols = slice(P * k, P * (k + 1))
            c0_ps = psum.tile([P, Q], F32, name="c0_ps%d" % k)
            nc.tensor.matmul_mx(
                out=c0_ps[:], lhsT=val_codes[:, cols].bitcast(FP8X4), lhsT_scale=val_scales[:, cols],
                rhs=gout_codes[:].bitcast(FP8X4), rhs_scale=gout_scales[:], start=True, stop=True,
            )
            nc.scalar.activation(cs_turned[:, k, :], c0_ps[:], ACT.Copy, scale=size_cols[:, k : k + 1])
        for k in range(4):
            nc.tensor.transpose(cs_ps[:, P * k : P * (k + 1)], cs_turned[:, k, :], ident[:])

        ta_sum = shared.tile([P, G], F32, name="ta_sum", offset=AT_VAL_POOL, align_bytes=64)
        nc.vector.tensor_reduce(ta_sum[:], by_span(ta_ps[:]), AX.X, ALU.add)
        inv_z = keep.tile([P, 1], F32, name="inv_z")
        nc.vector.reciprocal(inv_z[:], z[:])
        ta_t = shared.tile([P, I], F32, name="ta_t", offset=AT_GOUT_GROUPED, align_bytes=64)
        nc.gpsimd.tensor_tensor(ta_t[:], ta_sb[:], t[:], ALU.mult)
        r_ta = keep.tile([P, G], F32, name="r_ta")
        mean_sum = keep.tile([P, 1], F32, name="mean_sum")
        nc.vector.scalar_tensor_tensor(
            r_ta[:], ta_sum[:], inv_z[:], p[:], ALU.mult, ALU.mult, accum_out=mean_sum[:]
        )
        centred = keep.tile([P, G], F32, name="centred")
        nc.vector.tensor_scalar(centred[:], ta_sum[:], mean_sum[:], 1.0 / SPAN, ALU.subtract, ALU.mult)
        share = keep.tile([P, I], F32, name="share")
        nc.scalar.activation(by_span(share[:]), over_span(p[:]), ACT.Copy, scale=inv_z[:])
        bend = keep.tile([P, I], F32, name="bend")
        nc.gpsimd.tensor_tensor(by_span(bend[:]), by_span(ta_t[:]), over_span(centred[:]), ALU.subtract)

        drr2 = keep.tile([P, I], F32, name="drr2")
        nc.vector.scalar_tensor_tensor(drr2[:], t[:], 1.0, cs_ps[:], ALU.add, ALU.mult)
        slope = keep.tile([P, I], F32, name="slope")
        nc.vector.scalar_tensor_tensor(slope[:], tsq4[:], 4.0, cs_ps[:], ALU.subtract, ALU.mult)
        dr2 = keep.tile([P, G], F32, name="dr2")
        nc.vector.tensor_reduce(dr2[:], by_span(drr2[:]), AX.X, ALU.add)
        tdrr = keep.tile([P, I], F32, name="tdrr")
        nc.vector.tensor_tensor(tdrr[:], ta_ps[:], slope[:], ALU.mult)
        r_dr = keep.tile([P, G], F32, name="r_dr")
        mean_dr = keep.tile([P, 1], F32, name="mean_dr")
        nc.vector.scalar_tensor_tensor(
            r_dr[:], dr2[:], inv_z[:], p[:], ALU.mult, ALU.mult, accum_out=mean_dr[:]
        )
        tdr = keep.tile([P, G], F32, name="tdr")
        nc.vector.tensor_reduce(tdr[:], by_span(tdrr[:]), AX.X, ALU.add)
        cross = keep.tile([P, G], F32, name="cross")
        nc.vector.scalar_tensor_tensor(cross[:], dr2[:], mean_dr[:], centred[:], ALU.subtract, ALU.mult)
        w = keep.tile([P, G], F32, name="w")
        nc.vector.scalar_tensor_tensor(w[:], tdr[:], -0.125, cross[:], ALU.mult, ALU.add)
        local = keep.tile([P, I], F32, name="local")
        nc.gpsimd.tensor_tensor(local[:], slope[:], bend[:], ALU.mult)
        r_w = keep.tile([P, G], F32, name="r_w")
        mean_w = keep.tile([P, 1], F32, name="mean_w")
        nc.vector.scalar_tensor_tensor(
            r_w[:], w[:], inv_z[:], p[:], ALU.mult, ALU.mult, accum_out=mean_w[:]
        )
        total = keep.tile([P, I], F32, name="total")
        nc.vector.scalar_tensor_tensor(
            by_span(total[:]), over_span(w[:]), mean_w[:], by_span(local[:]), ALU.subtract, ALU.add
        )
        nc.vector.tensor_tensor(window[:].indirect(offsets[:]), total[:], share[:], ALU.mult)

        start = 0
        for width in OUT_CHUNKS:
            cols = slice(start, start + width)
            result = keep.tile([P, width], F32, name="result%d" % start)
            nc.vector.tensor_tensor(result[:], window[:, cols], base_sb[:, cols], ALU.add)
            nc.sync.dma_start(out=out[:, cols], in_=result[:])
            start = start + width
